import numpy as np
import ml_dtypes


def mxq(x, axis, fmt="e4m3"):
    dtype, down = {"e4m3": (ml_dtypes.float8_e4m3fn, 7), "e5m2": (ml_dtypes.float8_e5m2, 14)}[fmt]
    v = np.moveaxis(np.asarray(x, np.float32).astype(ml_dtypes.bfloat16).astype(np.float64), axis, -1)
    blocks = v.reshape(v.shape[:-1] + (-1, 32))
    amax = np.abs(blocks).max(-1, keepdims=True)
    byte = np.maximum(np.where(amax > 0, np.frexp(amax)[1] - 1 + 127, 0) - down, 1)
    scale = np.exp2(byte - 127.0)
    codes = (blocks / scale).astype(np.float32).astype(dtype).astype(np.float64)
    return np.moveaxis((codes * scale).reshape(v.shape), -1, axis)


WIDE = False


def mx_kscale(k):
    if not WIDE:
        return np.ones(k)
    levels = np.array([10, -10, 5, -5, 0])
    if k % 512:
        return np.exp2(np.random.permutation(np.resize(levels, k // 32))).repeat(32)
    a = np.empty((k // 512, 16))
    for p in range(k // 512):
        a[p, :8] = np.random.permutation(np.resize(levels, 8))
        for g in range(8):
            far = levels[np.abs(levels - a[p, g]) >= 10]
            a[p, g + 8] = far[np.random.randint(len(far))]
    return np.exp2(a.ravel()).repeat(32)


def f64(x):
    return np.asarray(x).astype(np.float64)


def striped(idx):
    return np.tile(idx.reshape(-1, 16).T, (8, 1)).astype(np.uint16)


def unstriped(offs):
    return offs[:16].T.reshape(-1).astype(np.int64)


E2M1 = np.array([0.0, 0.5, 1.0, 1.5, 2.0, 3.0, 4.0, 6.0, -0.0, -0.5, -1.0, -1.5, -2.0, -3.0, -4.0, -6.0])


def pack_weight(w, fmt):
    k, n = w.shape
    w = f64(np.asarray(w, np.float32).astype(ml_dtypes.bfloat16)).reshape(k // 32, 32, n)
    amax = np.abs(w).max(1)
    if fmt == "e4m3":
        byte = np.frexp(amax)[1] - 1 + 127 - 7
    else:
        mant, ex = np.frexp(amax / 6.0)
        byte = np.where(mant > 0.5, ex, ex - 1) + 127
    byte = np.clip(np.where(amax > 0, byte, 1), 1, 254)
    scaled = (w * np.exp2(127.0 - byte)[:, None, :]).reshape(k, n).astype(np.float32)
    by_word = np.ascontiguousarray(scaled.reshape(k // 512, 128, 4, n).transpose(0, 1, 3, 2))
    if fmt == "e4m3":
        words = by_word.astype(ml_dtypes.float8_e4m3fn).view(np.uint8)
    else:
        c = by_word.astype(ml_dtypes.float4_e2m1fn).view(np.uint8) & 0xF
        words = (c[..., 0::2] | (c[..., 1::2] << 4)).reshape(k // 512, 128, 2 * n)
    return np.ascontiguousarray(words), np.ascontiguousarray(byte.astype(np.uint8).reshape(k // 512, 16, n))


def unpack_weight(words, scales, fmt):
    g, _, n = scales.shape
    words = np.ascontiguousarray(words).reshape(g, 128, n, -1)
    if fmt == "e4m3":
        vals = words.view(ml_dtypes.float8_e4m3fn).astype(np.float64)
    else:
        nib = np.empty((g, 128, n, 4), np.uint8)
        nib[..., 0::2] = words & 0xF
        nib[..., 1::2] = words >> 4
        vals = E2M1[nib]
    vals = vals * np.repeat(np.exp2(scales.astype(np.float64) - 127.0), 8, axis=1)[..., None]
    return vals.transpose(0, 1, 3, 2).reshape(g * 512, n)


def gelu(v):
    return 0.5 * v * (1.0 + np.tanh(np.sqrt(2.0 / np.pi) * (v + 0.044715 * v**3)))


def striped8(idx):
    return np.concatenate([v.reshape(-1, 16).T for v in idx]).astype(np.uint16)


def unstriped8(offs):
    return np.stack([offs[16 * g:16 * g + 16].T.reshape(-1) for g in range(8)]).astype(np.int64)


def put_heads(h, wgs, idx8, t2):
    r = np.arange(h.shape[0])
    page = np.zeros((h.shape[0], t2))
    page[r[:, None], idx8[r % 512 // 64]] = wgs[r // 4 % 128] * h
    return page


def bf(x):
    return np.asarray(x, np.float32).astype(ml_dtypes.bfloat16)


def planes(Y):
    n, m = Y.shape
    b = f64(bf(Y)).reshape(n // 32, 32, m)
    amax = np.abs(b).max(1)
    byte = np.clip(np.where(amax > 0, np.frexp(amax)[1] - 1 + 127 - 7, 1), 1, 254)
    codes = (b * np.exp2(127.0 - byte)[:, None, :]).reshape(n, m).astype(np.float32).astype(ml_dtypes.float8_e4m3fn).view(np.uint8)
    words = codes.reshape(n // 512, 128, 4, m).transpose(0, 1, 3, 2)
    return np.ascontiguousarray(words), np.ascontiguousarray(byte.astype(np.uint8).reshape(n // 512, 16, m))


K, T, S, T2, H, N = 1536, 2048, 512, 1024, 1024, 1024

def setup_inputs():
    n = np.random.standard_normal
    s = mx_kscale(K)[:, None]
    u = mx_kscale(H)[:, None]
    size = np.sqrt(np.exp(0.8 * n(N)))
    tab_words, tab_scales = pack_weight(n((K, T)) * s, "e4m3")
    w3_words, w3_scales = pack_weight(n((H, N)) / u * size[None, :] / np.sqrt(H), "e2m1")
    return {
        "tab_words": tab_words, "tab_scales": tab_scales,
        "offs": striped(np.random.permutation(T)[:S]),
        "w1": (n((K, H)) / s * u.T / np.sqrt(K)).astype(np.float32),
        "lo": (-(0.4 + 0.6 * np.random.uniform(size=H)) * u[:, 0]).astype(np.float32),
        "hi": ((0.6 + 0.8 * np.random.uniform(size=H)) * u[:, 0]).astype(np.float32),
        "wgs": np.repeat(np.random.uniform(0.5, 2.0, (8, S)), 16, axis=0).astype(np.float32),
        "offs2": striped8(np.stack([np.random.permutation(T2)[:S] for _ in range(8)])),
        "committed": (0.8 * n((H, T2)) * u).astype(np.float32),
        "w3_words": w3_words, "w3_scales": w3_scales,
        "quota": ((0.5 * n((N, T2)) - 0.7) * size[:, None]).astype(np.float32),
        "least": ((0.4 + 0.3 * np.random.uniform(size=N)) * size).astype(np.float32),
    }

def reference(tab_words, tab_scales, offs, w1, lo, hi, wgs, offs2, committed,
              w3_words, w3_scales, quota, least):
    v = unpack_weight(tab_words, tab_scales, "e4m3")[:, unstriped(offs)]
    a = mxq(f64(w1), 0, "e4m3").T @ v
    h = np.minimum(np.maximum(a, f64(lo)[:, None]), f64(hi)[:, None])
    page = put_heads(h, f64(wgs), unstriped8(offs2), T2)
    z = page + f64(committed)
    w3 = unpack_weight(w3_words, w3_scales, "e2m1")
    d = (w3.T @ mxq(z, 0, "e4m3")) - f64(quota)
    y = np.square(np.maximum(d, f64(least)[:, None]))
    words, scales = planes(y)
    return y, words, scales

@@ -1,0 +1,361 @@
+from contextlib import ExitStack
+
+import concourse.mybir as mybir
+from concourse.masks import make_identity
+
+K, T, S, T2, H, N = 1536, 2048, 512, 1024, 1024, 1024
+FLOPS = 2 * K * H * S + 2 * H * N * T2
+
+F32 = mybir.dt.float32
+BF16 = mybir.dt.bfloat16
+I32 = mybir.dt.int32
+U32 = mybir.dt.uint32
+U16 = mybir.dt.uint16
+U8 = mybir.dt.uint8
+FP8X4 = mybir.dt.float8_e4m3fn_x4
+FP4X4 = mybir.dt.float4_e2m1fn_x4
+ALU = mybir.AluOpType
+ACT = mybir.ActivationFunctionType
+
+P = 128
+PACK = 4
+KP = P * PACK
+BANK = 512
+PAGES = 4
+
+
+def tile_list_quota_penalty_scores_kernel(
+    tc, tab_words, tab_scales, offs, w1, lo, hi, wgs, offs2, committed,
+    w3_words, w3_scales, quota, least, out_0, out_1, out_2,
+):
+    nc = tc.nc
+    passes1 = K // KP
+    groups = H // KP
+    halves = T2 // BANK
+
+    with ExitStack() as ctx:
+        keep = ctx.enter_context(tc.tile_pool(name="keep", bufs=1))
+        ring = ctx.enter_context(tc.tile_pool(name="ring", bufs=1))
+        psum = ctx.enter_context(tc.psum_pool(name="psum", bufs=1))
+
+        offs_t = keep.tile([P, S // 16], U16, name="offs_t")
+        offs2_t = keep.tile([P, S // 16], U16, name="offs2_t")
+        tab_s = keep.tile([P, T], U8, name="tab_s", align_bytes=64)
+        w3_s = keep.tile([P, groups * N], U8, name="w3_s", align_bytes=64)
+        w3_w = keep.tile([P, groups * 2 * N], U8, name="w3_w", align_bytes=64)
+        w3_sp = keep.tile([P, groups * N], U8, name="w3_sp", align_bytes=64)
+        w3_wp = keep.tile([P, groups * 2 * N], U8, name="w3_wp", align_bytes=64)
+        lo_t = keep.tile([P, 8], F32, name="lo_t")
+        hi_t = keep.tile([P, 8], F32, name="hi_t")
+        least_t = keep.tile([P, 8], F32, name="least_t")
+        nleast_t = keep.tile([P, 8], F32, name="nleast_t")
+        wgs_t = keep.tile([P, S], F32, name="wgs_t")
+        tab_w = [keep.tile([P, T], U32, name="tab_w%d" % a, align_bytes=64) for a in range(passes1)]
+        v_w = [keep.tile([P, S], U32, name="v_w%d" % a, align_bytes=64) for a in range(passes1)]
+        v_s = keep.tile([P, S], U8, name="v_s", align_bytes=64)
+        pages = [keep.tile([P, T2], F32, name="page%d" % i) for i in range(PAGES)]
+        y_s = keep.tile([P, groups * T2], U8, name="y_s", align_bytes=64)
+
+        nc.gpsimd.memset(tab_s[:].bitcast(I32), 0)
+        nc.gpsimd.memset(w3_s[:].bitcast(I32), 0)
+        ident = keep.tile([P, P], F32, name="ident")
+        make_identity(nc, ident[:])
+        for page in pages:
+            nc.gpsimd.memset(page[:], 0.0)
+
+        def load_tab(a):
+            nc.sync.dma_start(out=tab_w[a][:].bitcast(I32),
+                              in_=tab_words[a].rearrange("p t i -> p (t i)").bitcast(I32))
+
+        w1_raw = {}
+
+        def load_w1(a, b):
+            raw = ring.tile([P, PACK, KP], F32, tag="wq", bufs=5, name="w1_raw")
+            nc.sync.dma_start(out=raw[:], in_=w1[KP * a:KP * (a + 1), KP * b:KP * (b + 1)]
+                              .rearrange("(p j) c -> p j c", j=PACK))
+            w1_raw[(a, b)] = raw
+
+        def load_vec(tile, vec):
+            nc.sync.dma_start(out=tile[:].rearrange("p (b t) -> p b t", t=PACK),
+                              in_=vec.rearrange("(b p t) -> p b t", p=P, t=PACK))
+
+        def load_tab_scales(q):
+            nc.sync.dma_start(out=tab_s[32 * q:32 * q + 4 * passes1, :].bitcast(I32),
+                              in_=tab_scales[:, 4 * q:4 * q + 4, :].bitcast(I32))
+
+        def load_w3_scales(q):
+            nc.sync.dma_start(out=w3_s[32 * q:32 * q + 4, :].bitcast(I32).rearrange("r (a n) -> r a n", a=groups),
+                              in_=w3_scales[:, 4 * q:4 * q + 4, :].bitcast(I32).rearrange("a r n -> r a n"))
+
+        nc.sync.dma_start(offs_t[:], offs)
+        load_tab(0)
+        nc.sync.dma_start(out=w3_w[:].bitcast(I32).rearrange("p (a n) -> p a n", a=groups),
+                          in_=w3_words.bitcast(I32).rearrange("a p n -> p a n"))
+        load_vec(least_t, least)
+        nc.sync.dma_start(offs2_t[:], offs2)
+        load_vec(lo_t, lo)
+        load_vec(hi_t, hi)
+        load_w1(0, 0)
+        load_tab_scales(0)
+        load_tab_scales(1)
+        load_tab_scales(2)
+        load_tab_scales(3)
+        load_tab(1)
+        for q in range(4):
+            load_w3_scales(q)
+        load_w1(1, 0)
+        load_tab(2)
+        w1_last = []
+        for hf in range(2):
+            raw = ring.tile([P, PACK, KP // 2], F32, tag="wl", bufs=2, name="w1_last")
+            nc.sync.dma_start(out=raw[:], in_=w1[KP * 2:KP * 3, 256 * hf:256 * (hf + 1)]
+                              .rearrange("(p j) c -> p j c", j=PACK))
+            w1_last.append(raw)
+        nc.sync.dma_start(out=wgs_t[:], in_=wgs)
+
+        com = {}
+
+        def load_com(b, u):
+            tile = ring.tile([P, 2, T2], F32, tag="cy", bufs=4, name="com")
+            nc.sync.dma_start(out=tile[:], in_=committed[KP * b:KP * (b + 1), :]
+                              .rearrange("(p t) m -> p t m", t=PACK)[:, 2 * u:2 * u + 2, :])
+            com[(b, u)] = tile
+
+        for a in range(passes1):
+            load_w1(a, 1)
+        load_com(0, 0)
+        load_com(0, 1)
+        load_com(1, 0)
+        load_com(1, 1)
+
+        nc.scalar.activation(out=nleast_t[:], in_=least_t[:], func=ACT.Identity, scale=-1.0)
+
+        def gather(a):
+            nc.vector.tensor_copy(out=v_w[a][:], in_=tab_w[a][:].indirect(offs_t[:]))
+
+        w1_q = {}
+
+        def quant_w1(a, b, split):
+            tag = {(0, 1): "hold2", (2, 1): "hold3"}.get((a, b), "grp")
+            grouped = ring.tile([P, PACK * KP], BF16, tag=tag, bufs=3 if tag == "grp" else 1, name="w1_grp", align_bytes=64)
+            dst = grouped[:].rearrange("p (t m j) -> p m j t", t=PACK, j=PACK)
+            srcv = w1_raw[(a, b)][:].rearrange("p j (m t) -> p m j t", t=PACK)
+            if split < P:
+                nc.vector.tensor_copy(out=dst[:, split:], in_=srcv[:, split:])
+            nc.scalar.copy(out=dst[:, :split], in_=srcv[:, :split])
+            codes = keep.tile([P, KP], U32, name="w1_c%d%d" % (a, b), align_bytes=64)
+            scales = keep.tile([P, KP], U8, name="w1_s%d%d" % (a, b), align_bytes=64)
+            nc.vector.quantize_mx(out=codes[:].bitcast(FP8X4), scales=scales[:], in_=grouped[:])
+            w1_q[(a, b)] = (codes, scales)
+
+        def first_pass(acc, a, b, t):
+            codes, scales = w1_q[(a, b)]
+            nc.tensor.matmul_mx(out=acc[:], lhsT=codes[:, P * t:P * (t + 1)].bitcast(FP8X4),
+                                lhsT_scale=scales[:, P * t:P * (t + 1)],
+                                rhs=v_w[a][:].bitcast(FP8X4), rhs_scale=v_s[4 * a:P, :],
+                                start=(a == 0), stop=(a == passes1 - 1))
+
+        gather(0)
+        nc.vector.tensor_copy(
+            out=w3_wp[:].rearrange("p (g t m e) -> p g t m e", t=PACK, m=P, e=2),
+            in_=w3_w[:].rearrange("p (g m t e) -> p g t m e", t=PACK, m=P, e=2))
+        nc.vector.tensor_copy(out=v_s[:], in_=tab_s[:].indirect(offs_t[:]))
+        quant_w1(0, 0, P)
+        gather(1)
+        nc.vector.tensor_copy(
+            out=w3_sp[:].rearrange("p (g t m) -> p g t m", t=PACK, m=P),
+            in_=w3_s[:].rearrange("p (g m t) -> p g t m", t=PACK, m=P))
+        quant_w1(1, 0, P)
+        gather(2)
+        grouped = ring.tile([P, PACK * KP], BF16, tag="hold2", bufs=1, name="w1_grp", align_bytes=64)
+        dst = grouped[:].rearrange("p (t m j) -> p m j t", t=PACK, j=PACK)
+        src0 = w1_last[0][:].rearrange("p j (m t) -> p m j t", t=PACK)
+        src1 = w1_last[1][:].rearrange("p j (m t) -> p m j t", t=PACK)
+        nc.scalar.copy(out=dst[:, :64], in_=src0)
+        nc.vector.tensor_copy(out=dst[:, 84:], in_=src1[:, 20:])
+        nc.scalar.copy(out=dst[:, 64:84], in_=src1[:, :20])
+        codes = keep.tile([P, KP], U32, name="w1_c20", align_bytes=64)
+        scales = keep.tile([P, KP], U8, name="w1_s20", align_bytes=64)
+        for lo_c, hi_c in ((0, P), (P, 2 * P), (2 * P, KP)):
+            nc.vector.quantize_mx(out=codes[:, lo_c:hi_c].bitcast(FP8X4), scales=scales[:, lo_c:hi_c],
+                                  in_=grouped[:, PACK * lo_c:PACK * hi_c])
+        w1_q[(2, 0)] = (codes, scales)
+
+        z_q = {}
+        accs2 = {}
+        bank_tags = ["C", "C", "A", "A", "A", "A", "B", "B"]
+
+        def bank(tag, name):
+            return psum.tile([P, BANK], F32, tag=tag, bufs=4 if tag == "A" else 2, name=name)
+
+        def second_pass(g, t, mh, b):
+            if b == 0:
+                accs2[(g, t, mh)] = bank(bank_tags[len(accs2) % 8], "acc2")
+            codes, scales = z_q[(b, mh)]
+            col = (b * groups + g) * KP + t * P
+            nc.tensor.matmul_mx(out=accs2[(g, t, mh)][:], lhsT=w3_wp[:, 2 * col:2 * (col + P)].bitcast(FP4X4),
+                                lhsT_scale=w3_sp[:, col:col + P],
+                                rhs=codes[:].bitcast(FP8X4), rhs_scale=scales[:],
+                                start=(b == 0), stop=(b == groups - 1))
+
+        raws = {}
+
+        def evac(i, acc):
+            raw = ring.tile([P, S], F32, tag="raw", bufs=5, name="raw")
+            nc.scalar.copy(out=raw[:], in_=acc[:])
+            raws[i] = raw
+
+        def quant_z0(mq):
+            c0 = ring.tile([P, BANK], U32, tag="hold%d" % (5 + mq), bufs=1, name="z_c0", align_bytes=64)
+            s0 = keep.tile([P, BANK], U8, name="z_s0%d" % mq, align_bytes=64)
+            nc.vector.quantize_mx(out=c0[:].bitcast(FP8X4), scales=s0[:], in_=z_q[(0, mq)][:])
+            z_q[(0, mq)] = (c0, s0)
+
+        def post(i):
+            tag = {2: "hold2", 3: "hold3", 5: "hold5", 6: "hold6"}.get(i, "h")
+            h = ring.tile([P, S], F32, tag=tag, bufs=2 if tag == "h" else 1, name="h", align_bytes=64)
+            raw = raws[i]
+            nc.vector.tensor_scalar(out=h[:], in0=raw[:], scalar1=lo_t[:, i:i + 1], scalar2=hi_t[:, i:i + 1],
+                                    op0=ALU.max, op1=ALU.min)
+            nc.vector.tensor_tensor(out=pages[i % PAGES][:].indirect(offs2_t[:]), in0=h[:], in1=wgs_t[:], op=ALU.mult)
+
+        def turn(dst, srcv, start, stop):
+            nc.tensor.matmul(out=dst, lhsT=srcv, rhs=ident[:], start=start, stop=stop, is_transpose=True)
+
+        accs = [bank("A", "acc1") for t in range(PACK)]
+        for a in range(passes1):
+            for t in range(PACK):
+                first_pass(accs[t], a, 0, t)
+        raws[0] = accs[0]
+        for t in range(1, PACK):
+            evac(t, accs[t])
+        z_t = {}
+        for u in range(2):
+            for e in range(2):
+                t = 2 * u + e
+                if t == 2:
+                    quant_w1(0, 1, P)
+                if t == 3:
+                    quant_w1(1, 1, P)
+                    quant_w1(2, 1, P)
+                    for t1 in range(PACK):
+                        acc = bank("C", "acc1")
+                        for a in range(passes1):
+                            first_pass(acc, a, 1, t1)
+                        evac(PACK + t1, acc)
+                post(t)
+            sums = [bank("A", "sums") for jj in range(4)]
+            for jj in range(4):
+                for j in range(2):
+                    for e in range(2):
+                        mcols = slice(P * (2 * jj + j), P * (2 * jj + j + 1))
+                        turn(sums[jj][:, P * (2 * j + e):P * (2 * j + e + 1)], com[(0, u)][:, e, mcols],
+                             j == 0 and e == 0, False)
+            for e in range(2):
+                page = pages[(2 * u + e) % PAGES]
+                for jj in range(4):
+                    for j in range(2):
+                        mcols = slice(P * (2 * jj + j), P * (2 * jj + j + 1))
+                        turn(sums[jj][:, P * (2 * j + e):P * (2 * j + e + 1)], page[:, mcols],
+                             False, j == 1 and e == 1)
+            for jj in range(4):
+                zt = ring.tile([P, BANK], BF16, tag="zt", bufs=8, name="zt")
+                nc.scalar.copy(out=zt[:].rearrange("m (j p e) -> m j p e", j=2, e=2),
+                               in_=sums[jj][:].rearrange("m (j e p) -> m j p e", j=2, e=2))
+                z_t[(u, jj)] = zt
+        for mh in range(halves):
+            grouped = ring.tile([P, PACK * BANK], BF16, tag="grp", bufs=3, name="z_grp", align_bytes=64)
+            for jh in range(2):
+                jj = 2 * mh + jh
+                words = bank("B", "words")
+                for u in range(2):
+                    for j in range(2):
+                        turn(words[:, P * (2 * u + j):P * (2 * u + j + 1)],
+                             z_t[(u, jj)][:].bitcast(F32)[:, P * j:P * (j + 1)], True, True)
+                nc.scalar.copy(out=grouped[:].bitcast(F32)[:, BANK * jh:BANK * (jh + 1)].rearrange("p (m u) -> p m u", u=2),
+                               in_=words[:].rearrange("p (u m) -> p m u", u=2))
+            z_q[(0, mh)] = grouped
+
+        z4 = [keep.tile([P, PACK, BANK], BF16, name="z4_%d" % mh) for mh in range(halves)]
+
+        def add_com(t, mh):
+            cols = slice(BANK * mh, BANK * (mh + 1))
+            nc.vector.tensor_tensor(out=z4[mh][:, t, :], in0=pages[(PACK + t) % PAGES][:, cols],
+                                    in1=com[(1, t // 2)][:, t % 2, cols], op=ALU.add)
+
+        for t in range(PACK):
+            post(PACK + t)
+            if t < PACK - 1:
+                for mh in range(halves):
+                    add_com(t, mh)
+            if t in (1, 2):
+                quant_z0(t - 1)
+            if t == 1:
+                for g in range(groups):
+                    for t2 in range(PACK):
+                        second_pass(g, t2, 0, 0)
+        for mh in range(halves):
+            add_com(PACK - 1, mh)
+            grouped = ring.tile([P, PACK * BANK], BF16, tag="grp", bufs=3, name="z_grp", align_bytes=64)
+            dst = grouped[:].rearrange("p (c i t) -> p c t i", i=4, t=PACK)
+            srcv = z4[mh][:].rearrange("p t (c i) -> p c t i", i=4)
+            if mh == 0:
+                nc.vector.tensor_copy(out=dst[:, 40:], in_=srcv[:, 40:])
+                nc.scalar.copy(out=dst[:, :40], in_=srcv[:, :40])
+            else:
+                nc.scalar.copy(out=dst, in_=srcv)
+            codes = keep.tile([P, BANK], U32, name="z_c1%d" % mh, align_bytes=64)
+            scales = keep.tile([P, BANK], U8, name="z_s1%d" % mh, align_bytes=64)
+            nc.vector.quantize_mx(out=codes[:].bitcast(FP8X4), scales=scales[:], in_=grouped[:])
+            z_q[(1, mh)] = (codes, scales)
+
+        quo = {}
+        for mh in range(halves):
+            for g in range(groups):
+                tile = ring.tile([P, PACK, BANK], F32, tag="wq", bufs=5, name="quo")
+                nc.sync.dma_start(out=tile[:], in_=quota[KP * g:KP * (g + 1), BANK * mh:BANK * (mh + 1)]
+                                  .rearrange("(p t) m -> p t m", t=PACK))
+                quo[(g, mh)] = tile
+
+        def finish(g, mh, c0, width, on_vector, cast_split):
+            cols = slice(BANK * mh + c0, BANK * mh + c0 + width)
+            y = ring.tile([P, PACK, width], F32, tag="cy", bufs=4, name="y")
+            y_out = out_0[KP * g:KP * (g + 1), cols].rearrange("(p t) m -> p t m", t=PACK)
+            for t in range(PACK):
+                i = g * PACK + t
+                if c0 == 0:
+                    if (g, t, mh) not in accs2:
+                        second_pass(g, t, mh, 0)
+                    second_pass(g, t, mh, 1)
+                d = ring.tile([P, width], F32, tag="raw", bufs=5, name="d")
+                nc.vector.tensor_tensor(out=d[:], in0=accs2[(g, t, mh)][:, c0:c0 + width],
+                                        in1=quo[(g, mh)][:, t, c0:c0 + width], op=ALU.subtract)
+                r = ring.tile([P, width], F32, tag="r", bufs=3, name="r")
+                if t in on_vector:
+                    nc.vector.tensor_scalar(out=r[:], in0=d[:], scalar1=least_t[:, i:i + 1], scalar2=None, op0=ALU.max)
+                    nc.scalar.activation(out=y[:, t, :], in_=r[:], func=ACT.Square)
+                else:
+                    nc.scalar.activation(out=r[:], in_=d[:], func=ACT.Relu, bias=nleast_t[:, i:i + 1])
+                    nc.scalar.activation(out=y[:, t, :], in_=r[:], func=ACT.Square, bias=least_t[:, i:i + 1])
+                if t % 2 == 1:
+                    nc.sync.dma_start(out=y_out[:, t - 1:t + 1, :], in_=y[:, t - 1:t + 1, :])
+            grouped = ring.tile([P, PACK * width], BF16, tag="grp", bufs=3, name="y_grp", align_bytes=64)
+            dst = grouped[:].rearrange("p (c i t) -> p c t i", i=4, t=PACK)
+            srcv = y[:].rearrange("p t (c i) -> p c t i", i=4)
+            nc.vector.tensor_copy(out=dst[:, cast_split:], in_=srcv[:, cast_split:])
+            if cast_split > 0:
+                nc.scalar.copy(out=dst[:, :cast_split], in_=srcv[:, :cast_split])
+            codes = ring.tile([P, width], U32, tag="y_c", bufs=4, name="y_c", align_bytes=64)
+            scol = g * T2 + BANK * mh + c0
+            nc.vector.quantize_mx(out=codes[:].bitcast(FP8X4), scales=y_s[:, scol:scol + width], in_=grouped[:])
+            nc.sync.dma_start(out=out_1[g, :, cols, :].rearrange("p m i -> p (m i)").bitcast(I32),
+                              in_=codes[:].bitcast(I32))
+
+        finish(0, 0, 0, BANK, (0,), 0)
+        finish(1, 0, 0, BANK, (), 0)
+        finish(0, 1, 0, BANK, (), 0)
+        finish(1, 1, 0, BANK // 2, (), 0)
+        finish(1, 1, BANK // 2, BANK // 2, (3,), 20)
+        for q in range(4):
+            nc.sync.dma_start(out=out_2[:, 4 * q:4 * q + 4, :].bitcast(I32).rearrange("g r m -> r g m"),
+                              in_=y_s[32 * q:32 * q + 4, :].bitcast(I32).rearrange("r (g m) -> r g m", g=groups))

@@ -58,10 +58,8 @@ def tile_list_quota_penalty_scores_kernel(
 
         nc.gpsimd.memset(tab_s[:].bitcast(I32), 0)
         nc.gpsimd.memset(w3_s[:].bitcast(I32), 0)
-        ident = keep.tile([P, P], F32, name="ident")
-        make_identity(nc, ident[:])
         for page in pages:
-            nc.gpsimd.memset(page[:], 0.0)
+            nc.vector.memset(page[:], 0.0)
 
         def load_tab(a):
             nc.sync.dma_start(out=tab_w[a][:].bitcast(I32),
@@ -80,29 +78,25 @@ def tile_list_quota_penalty_scores_kernel(
                               in_=vec.rearrange("(b p t) -> p b t", p=P, t=PACK))
 
         def load_tab_scales(q):
-            nc.sync.dma_start(out=tab_s[32 * q:32 * q + 4 * passes1, :].bitcast(I32),
+            nc.gpsimd.dma_start(out=tab_s[32 * q:32 * q + 4 * passes1, :].bitcast(I32),
                               in_=tab_scales[:, 4 * q:4 * q + 4, :].bitcast(I32))
 
         def load_w3_scales(q):
-            nc.sync.dma_start(out=w3_s[32 * q:32 * q + 4, :].bitcast(I32).rearrange("r (a n) -> r a n", a=groups),
+            nc.gpsimd.dma_start(out=w3_s[32 * q:32 * q + 4, :].bitcast(I32).rearrange("r (a n) -> r a n", a=groups),
                               in_=w3_scales[:, 4 * q:4 * q + 4, :].bitcast(I32).rearrange("a r n -> r a n"))
 
         nc.sync.dma_start(offs_t[:], offs)
         load_tab(0)
         nc.sync.dma_start(out=w3_w[:].bitcast(I32).rearrange("p (a n) -> p a n", a=groups),
                           in_=w3_words.bitcast(I32).rearrange("a p n -> p a n"))
-        load_vec(least_t, least)
-        nc.sync.dma_start(offs2_t[:], offs2)
-        load_vec(lo_t, lo)
-        load_vec(hi_t, hi)
-        load_w1(0, 0)
-        load_tab_scales(0)
-        load_tab_scales(1)
-        load_tab_scales(2)
-        load_tab_scales(3)
-        load_tab(1)
+        for q in range(4):
+            load_tab_scales(q)
         for q in range(4):
             load_w3_scales(q)
+        ident = keep.tile([P, P], F32, name="ident")
+        make_identity(nc, ident[:])
+        load_w1(0, 0)
+        load_tab(1)
         load_w1(1, 0)
         load_tab(2)
         w1_last = []
@@ -111,7 +105,11 @@ def tile_list_quota_penalty_scores_kernel(
             nc.sync.dma_start(out=raw[:], in_=w1[KP * 2:KP * 3, 256 * hf:256 * (hf + 1)]
                               .rearrange("(p j) c -> p j c", j=PACK))
             w1_last.append(raw)
+        load_vec(lo_t, lo)
+        load_vec(hi_t, hi)
+        nc.sync.dma_start(offs2_t[:], offs2)
         nc.sync.dma_start(out=wgs_t[:], in_=wgs)
+        load_vec(least_t, least)
 
         com = {}
 
@@ -212,7 +210,7 @@ def tile_list_quota_penalty_scores_kernel(
             z_q[(0, mq)] = (c0, s0)
 
         def post(i):
-            tag = {2: "hold2", 3: "hold3", 5: "hold5", 6: "hold6"}.get(i, "h")
+            tag = {2: "hold2", 3: "hold3", 6: "hold5", 7: "hold6"}.get(i, "h")
             h = ring.tile([P, S], F32, tag=tag, bufs=2 if tag == "h" else 1, name="h", align_bytes=64)
             raw = raws[i]
             nc.vector.tensor_scalar(out=h[:], in0=raw[:], scalar1=lo_t[:, i:i + 1], scalar2=hi_t[:, i:i + 1],
@@ -276,29 +274,26 @@ def tile_list_quota_penalty_scores_kernel(
                                in_=words[:].rearrange("p (u m) -> p m u", u=2))
             z_q[(0, mh)] = grouped
 
-        z4 = [keep.tile([P, PACK, BANK], BF16, name="z4_%d" % mh) for mh in range(halves)]
+        z4 = keep.tile([P, PACK, T2], BF16, name="z4")
 
-        def add_com(t, mh):
-            cols = slice(BANK * mh, BANK * (mh + 1))
-            nc.vector.tensor_tensor(out=z4[mh][:, t, :], in0=pages[(PACK + t) % PAGES][:, cols],
+        def add_com(t, cols):
+            nc.vector.tensor_tensor(out=z4[:, t, cols], in0=pages[(PACK + t) % PAGES][:, cols],
                                     in1=com[(1, t // 2)][:, t % 2, cols], op=ALU.add)
 
         for t in range(PACK):
             post(PACK + t)
             if t < PACK - 1:
-                for mh in range(halves):
-                    add_com(t, mh)
-            if t in (1, 2):
-                quant_z0(t - 1)
-            if t == 1:
+                add_com(t, slice(0, T2))
+            if t == 2:
+                quant_z0(0)
                 for g in range(groups):
                     for t2 in range(PACK):
                         second_pass(g, t2, 0, 0)
         for mh in range(halves):
-            add_com(PACK - 1, mh)
+            add_com(PACK - 1, slice(BANK * mh, BANK * (mh + 1)))
             grouped = ring.tile([P, PACK * BANK], BF16, tag="grp", bufs=3, name="z_grp", align_bytes=64)
             dst = grouped[:].rearrange("p (c i t) -> p c t i", i=4, t=PACK)
-            srcv = z4[mh][:].rearrange("p t (c i) -> p c t i", i=4)
+            srcv = z4[:, :, BANK * mh:BANK * (mh + 1)].rearrange("p t (c i) -> p c t i", i=4)
             if mh == 0:
                 nc.vector.tensor_copy(out=dst[:, 40:], in_=srcv[:, 40:])
                 nc.scalar.copy(out=dst[:, :40], in_=srcv[:, :40])
@@ -308,6 +303,8 @@ def tile_list_quota_penalty_scores_kernel(
             scales = keep.tile([P, BANK], U8, name="z_s1%d" % mh, align_bytes=64)
             nc.vector.quantize_mx(out=codes[:].bitcast(FP8X4), scales=scales[:], in_=grouped[:])
             z_q[(1, mh)] = (codes, scales)
+            if mh == 0:
+                quant_z0(1)
 
         quo = {}
         for mh in range(halves):

@@ -56,8 +56,8 @@ def tile_list_quota_penalty_scores_kernel(
         pages = [keep.tile([P, T2], F32, name="page%d" % i) for i in range(PAGES)]
         y_s = keep.tile([P, groups * T2], U8, name="y_s", align_bytes=64)
 
-        nc.gpsimd.memset(tab_s[:].bitcast(I32), 0)
-        nc.gpsimd.memset(w3_s[:].bitcast(I32), 0)
+        nc.vector.memset(tab_s[:].bitcast(I32), 0)
+        nc.vector.memset(w3_s[:].bitcast(I32), 0)
         for page in pages:
             nc.vector.memset(page[:], 0.0)
 
@@ -78,25 +78,29 @@ def tile_list_quota_penalty_scores_kernel(
                               in_=vec.rearrange("(b p t) -> p b t", p=P, t=PACK))
 
         def load_tab_scales(q):
-            nc.gpsimd.dma_start(out=tab_s[32 * q:32 * q + 4 * passes1, :].bitcast(I32),
+            nc.sync.dma_start(out=tab_s[32 * q:32 * q + 4 * passes1, :].bitcast(I32),
                               in_=tab_scales[:, 4 * q:4 * q + 4, :].bitcast(I32))
 
         def load_w3_scales(q):
-            nc.gpsimd.dma_start(out=w3_s[32 * q:32 * q + 4, :].bitcast(I32).rearrange("r (a n) -> r a n", a=groups),
+            nc.sync.dma_start(out=w3_s[32 * q:32 * q + 4, :].bitcast(I32).rearrange("r (a n) -> r a n", a=groups),
                               in_=w3_scales[:, 4 * q:4 * q + 4, :].bitcast(I32).rearrange("a r n -> r a n"))
 
         nc.sync.dma_start(offs_t[:], offs)
         load_tab(0)
         nc.sync.dma_start(out=w3_w[:].bitcast(I32).rearrange("p (a n) -> p a n", a=groups),
                           in_=w3_words.bitcast(I32).rearrange("a p n -> p a n"))
-        for q in range(4):
-            load_tab_scales(q)
-        for q in range(4):
-            load_w3_scales(q)
         ident = keep.tile([P, P], F32, name="ident")
         make_identity(nc, ident[:])
+        load_vec(least_t, least)
+        nc.sync.dma_start(offs2_t[:], offs2)
+        load_vec(lo_t, lo)
+        load_vec(hi_t, hi)
         load_w1(0, 0)
+        for q in range(4):
+            load_tab_scales(q)
         load_tab(1)
+        for q in range(4):
+            load_w3_scales(q)
         load_w1(1, 0)
         load_tab(2)
         w1_last = []
@@ -105,11 +109,7 @@ def tile_list_quota_penalty_scores_kernel(
             nc.sync.dma_start(out=raw[:], in_=w1[KP * 2:KP * 3, 256 * hf:256 * (hf + 1)]
                               .rearrange("(p j) c -> p j c", j=PACK))
             w1_last.append(raw)
-        load_vec(lo_t, lo)
-        load_vec(hi_t, hi)
-        nc.sync.dma_start(offs2_t[:], offs2)
         nc.sync.dma_start(out=wgs_t[:], in_=wgs)
-        load_vec(least_t, least)
 
         com = {}
 
@@ -136,8 +136,8 @@ def tile_list_quota_penalty_scores_kernel(
         def quant_w1(a, b, split):
             tag = {(0, 1): "hold2", (2, 1): "hold3"}.get((a, b), "grp")
             grouped = ring.tile([P, PACK * KP], BF16, tag=tag, bufs=3 if tag == "grp" else 1, name="w1_grp", align_bytes=64)
-            dst = grouped[:].rearrange("p (t m j) -> p m j t", t=PACK, j=PACK)
-            srcv = w1_raw[(a, b)][:].rearrange("p j (m t) -> p m j t", t=PACK)
+            dst = grouped[:].rearrange("p (t m j) -> p m t j", t=PACK, j=PACK)
+            srcv = w1_raw[(a, b)][:].rearrange("p j (m t) -> p m t j", t=PACK)
             if split < P:
                 nc.vector.tensor_copy(out=dst[:, split:], in_=srcv[:, split:])
             nc.scalar.copy(out=dst[:, :split], in_=srcv[:, :split])
@@ -166,9 +166,9 @@ def tile_list_quota_penalty_scores_kernel(
         quant_w1(1, 0, P)
         gather(2)
         grouped = ring.tile([P, PACK * KP], BF16, tag="hold2", bufs=1, name="w1_grp", align_bytes=64)
-        dst = grouped[:].rearrange("p (t m j) -> p m j t", t=PACK, j=PACK)
-        src0 = w1_last[0][:].rearrange("p j (m t) -> p m j t", t=PACK)
-        src1 = w1_last[1][:].rearrange("p j (m t) -> p m j t", t=PACK)
+        dst = grouped[:].rearrange("p (t m j) -> p m t j", t=PACK, j=PACK)
+        src0 = w1_last[0][:].rearrange("p j (m t) -> p m t j", t=PACK)
+        src1 = w1_last[1][:].rearrange("p j (m t) -> p m t j", t=PACK)
         nc.scalar.copy(out=dst[:, :64], in_=src0)
         nc.vector.tensor_copy(out=dst[:, 84:], in_=src1[:, 20:])
         nc.scalar.copy(out=dst[:, 64:84], in_=src1[:, :20])
@@ -210,8 +210,8 @@ def tile_list_quota_penalty_scores_kernel(
             z_q[(0, mq)] = (c0, s0)
 
         def post(i):
-            tag = {2: "hold2", 3: "hold3", 6: "hold5", 7: "hold6"}.get(i, "h")
-            h = ring.tile([P, S], F32, tag=tag, bufs=2 if tag == "h" else 1, name="h", align_bytes=64)
+            tag = {3: "hold3", 6: "hold5", 7: "hold6"}.get(i, "h")
+            h = ring.tile([P, S], F32, tag=tag, bufs=3 if tag == "h" else 1, name="h", align_bytes=64)
             raw = raws[i]
             nc.vector.tensor_scalar(out=h[:], in0=raw[:], scalar1=lo_t[:, i:i + 1], scalar2=hi_t[:, i:i + 1],
                                     op0=ALU.max, op1=ALU.min)

@@ -68,7 +68,8 @@ def tile_list_quota_penalty_scores_kernel(
         w1_raw = {}
 
         def load_w1(a, b):
-            raw = ring.tile([P, PACK, KP], F32, tag="wq", bufs=5, name="w1_raw")
+            last = (a, b) == (passes1 - 1, 1)
+            raw = ring.tile([P, PACK, KP], F32, tag="hold_w" if last else "wq", bufs=1 if last else 4, name="w1_raw")
             nc.sync.dma_start(out=raw[:], in_=w1[KP * a:KP * (a + 1), KP * b:KP * (b + 1)]
                               .rearrange("(p j) c -> p j c", j=PACK))
             w1_raw[(a, b)] = raw
@@ -119,9 +120,9 @@ def tile_list_quota_penalty_scores_kernel(
                               .rearrange("(p t) m -> p t m", t=PACK)[:, 2 * u:2 * u + 2, :])
             com[(b, u)] = tile
 
+        load_com(0, 0)
         for a in range(passes1):
             load_w1(a, 1)
-        load_com(0, 0)
         load_com(0, 1)
         load_com(1, 0)
         load_com(1, 1)
@@ -199,7 +200,7 @@ def tile_list_quota_penalty_scores_kernel(
         raws = {}
 
         def evac(i, acc):
-            raw = ring.tile([P, S], F32, tag="raw", bufs=5, name="raw")
+            raw = ring.tile([P, S], F32, tag="raw", bufs=5, name="raw", align_bytes=64)
             nc.scalar.copy(out=raw[:], in_=acc[:])
             raws[i] = raw
 
@@ -210,7 +211,7 @@ def tile_list_quota_penalty_scores_kernel(
             z_q[(0, mq)] = (c0, s0)
 
         def post(i):
-            tag = {3: "hold3", 6: "hold5", 7: "hold6"}.get(i, "h")
+            tag = {3: "hold3", 6: "hold5"}.get(i, "h")
             h = ring.tile([P, S], F32, tag=tag, bufs=3 if tag == "h" else 1, name="h", align_bytes=64)
             raw = raws[i]
             nc.vector.tensor_scalar(out=h[:], in0=raw[:], scalar1=lo_t[:, i:i + 1], scalar2=hi_t[:, i:i + 1],
@@ -228,6 +229,48 @@ def tile_list_quota_penalty_scores_kernel(
         for t in range(1, PACK):
             evac(t, accs[t])
         z_t = {}
+        sums = {}
+
+        def block(jj, j):
+            return slice(P * (2 * jj + j), P * (2 * jj + j + 1))
+
+        def turn_com(b, u, jjs):
+            for jj in jjs:
+                sums[jj] = bank("A", "sums")
+                for j in range(2):
+                    for e in range(2):
+                        turn(sums[jj][:, P * (2 * j + e):P * (2 * j + e + 1)], com[(b, u)][:, e, block(jj, j)],
+                             j == 0 and e == 0, False)
+
+        def turn_page(b, u, e, jjs):
+            page = pages[(PACK * b + 2 * u + e) % PAGES]
+            for jj in jjs:
+                for j in range(2):
+                    turn(sums[jj][:, P * (2 * j + e):P * (2 * j + e + 1)], page[:, block(jj, j)],
+                         False, j == 1 and e == 1)
+
+        def round_sums(b, u, jjs):
+            first = (b, u) == (0, 0)
+            zt = ring.tile([P, BANK * len(jjs)], BF16, tag="hold_w" if first else "zt", bufs=1 if first else 2, name="zt")
+            for k, jj in enumerate(jjs):
+                part = zt[:, BANK * k:BANK * (k + 1)]
+                nc.scalar.copy(out=part.rearrange("m (j p e) -> m j p e", j=2, e=2),
+                               in_=sums[jj][:].rearrange("m (j e p) -> m j p e", j=2, e=2))
+                z_t[(u, jj)] = part
+
+        def turn_back(mh):
+            grouped = ring.tile([P, PACK * BANK], BF16, tag="grp", bufs=3, name="z_grp", align_bytes=64)
+            for jh in range(2):
+                jj = 2 * mh + jh
+                words = bank("B", "words")
+                for u in range(2):
+                    for j in range(2):
+                        turn(words[:, P * (2 * u + j):P * (2 * u + j + 1)],
+                             z_t[(u, jj)].bitcast(F32)[:, P * j:P * (j + 1)], True, True)
+                nc.scalar.copy(out=grouped[:].bitcast(F32)[:, BANK * jh:BANK * (jh + 1)].rearrange("p (m u) -> p m u", u=2),
+                               in_=words[:].rearrange("p (u m) -> p m u", u=2))
+            return grouped
+
         for u in range(2):
             for e in range(2):
                 t = 2 * u + e
@@ -242,74 +285,46 @@ def tile_list_quota_penalty_scores_kernel(
                             first_pass(acc, a, 1, t1)
                         evac(PACK + t1, acc)
                 post(t)
-            sums = [bank("A", "sums") for jj in range(4)]
-            for jj in range(4):
-                for j in range(2):
-                    for e in range(2):
-                        mcols = slice(P * (2 * jj + j), P * (2 * jj + j + 1))
-                        turn(sums[jj][:, P * (2 * j + e):P * (2 * j + e + 1)], com[(0, u)][:, e, mcols],
-                             j == 0 and e == 0, False)
+            turn_com(0, u, range(4))
             for e in range(2):
-                page = pages[(2 * u + e) % PAGES]
-                for jj in range(4):
-                    for j in range(2):
-                        mcols = slice(P * (2 * jj + j), P * (2 * jj + j + 1))
-                        turn(sums[jj][:, P * (2 * j + e):P * (2 * j + e + 1)], page[:, mcols],
-                             False, j == 1 and e == 1)
-            for jj in range(4):
-                zt = ring.tile([P, BANK], BF16, tag="zt", bufs=8, name="zt")
-                nc.scalar.copy(out=zt[:].rearrange("m (j p e) -> m j p e", j=2, e=2),
-                               in_=sums[jj][:].rearrange("m (j e p) -> m j p e", j=2, e=2))
-                z_t[(u, jj)] = zt
+                turn_page(0, u, e, range(4))
+            round_sums(0, u, range(4))
         for mh in range(halves):
-            grouped = ring.tile([P, PACK * BANK], BF16, tag="grp", bufs=3, name="z_grp", align_bytes=64)
-            for jh in range(2):
-                jj = 2 * mh + jh
-                words = bank("B", "words")
-                for u in range(2):
-                    for j in range(2):
-                        turn(words[:, P * (2 * u + j):P * (2 * u + j + 1)],
-                             z_t[(u, jj)][:].bitcast(F32)[:, P * j:P * (j + 1)], True, True)
-                nc.scalar.copy(out=grouped[:].bitcast(F32)[:, BANK * jh:BANK * (jh + 1)].rearrange("p (m u) -> p m u", u=2),
-                               in_=words[:].rearrange("p (u m) -> p m u", u=2))
-            z_q[(0, mh)] = grouped
+            z_q[(0, mh)] = turn_back(mh)
 
-        z4 = keep.tile([P, PACK, T2], BF16, name="z4")
-
-        def add_com(t, cols):
-            nc.vector.tensor_tensor(out=z4[:, t, cols], in0=pages[(PACK + t) % PAGES][:, cols],
-                                    in1=com[(1, t // 2)][:, t % 2, cols], op=ALU.add)
-
+        z4 = keep.tile([P, PACK, BANK], BF16, name="z4")
+        late = (2, 3)
         for t in range(PACK):
+            u, e = divmod(t, 2)
             post(PACK + t)
-            if t < PACK - 1:
-                add_com(t, slice(0, T2))
+            nc.vector.tensor_tensor(out=z4[:, t, :], in0=pages[(PACK + t) % PAGES][:, 0:BANK],
+                                    in1=com[(1, u)][:, e, 0:BANK], op=ALU.add)
+            if t == PACK - 1:
+                grouped = ring.tile([P, PACK * BANK], BF16, tag="hold6", bufs=1, name="z_grp", align_bytes=64)
+                dst = grouped[:].rearrange("p (m t) -> p m t", t=PACK)
+                srcv = z4[:].rearrange("p t m -> p m t")
+                nc.vector.tensor_copy(out=dst[:, 160:], in_=srcv[:, 160:])
+                nc.scalar.copy(out=dst[:, :160], in_=srcv[:, :160])
+                codes = keep.tile([P, BANK], U32, name="z_c10", align_bytes=64)
+                scales = keep.tile([P, BANK], U8, name="z_s10", align_bytes=64)
+                nc.vector.quantize_mx(out=codes[:].bitcast(FP8X4), scales=scales[:], in_=grouped[:])
+                z_q[(1, 0)] = (codes, scales)
+                quant_z0(1)
+            if e == 0:
+                turn_com(1, u, late)
+            turn_page(1, u, e, late)
+            if e == 1:
+                round_sums(1, u, late)
             if t == 2:
                 quant_z0(0)
-                for g in range(groups):
-                    for t2 in range(PACK):
-                        second_pass(g, t2, 0, 0)
-        for mh in range(halves):
-            add_com(PACK - 1, slice(BANK * mh, BANK * (mh + 1)))
-            grouped = ring.tile([P, PACK * BANK], BF16, tag="grp", bufs=3, name="z_grp", align_bytes=64)
-            dst = grouped[:].rearrange("p (c i t) -> p c t i", i=4, t=PACK)
-            srcv = z4[:, :, BANK * mh:BANK * (mh + 1)].rearrange("p t (c i) -> p c t i", i=4)
-            if mh == 0:
-                nc.vector.tensor_copy(out=dst[:, 40:], in_=srcv[:, 40:])
-                nc.scalar.copy(out=dst[:, :40], in_=srcv[:, :40])
-            else:
-                nc.scalar.copy(out=dst, in_=srcv)
-            codes = keep.tile([P, BANK], U32, name="z_c1%d" % mh, align_bytes=64)
-            scales = keep.tile([P, BANK], U8, name="z_s1%d" % mh, align_bytes=64)
-            nc.vector.quantize_mx(out=codes[:].bitcast(FP8X4), scales=scales[:], in_=grouped[:])
-            z_q[(1, mh)] = (codes, scales)
-            if mh == 0:
-                quant_z0(1)
+                for t2 in range(PACK):
+                    second_pass(0, t2, 0, 0)
+        z_late = turn_back(1)
 
         quo = {}
         for mh in range(halves):
             for g in range(groups):
-                tile = ring.tile([P, PACK, BANK], F32, tag="wq", bufs=5, name="quo")
+                tile = ring.tile([P, PACK, BANK], F32, tag="wq", bufs=4, name="quo")
                 nc.sync.dma_start(out=tile[:], in_=quota[KP * g:KP * (g + 1), BANK * mh:BANK * (mh + 1)]
                                   .rearrange("(p t) m -> p t m", t=PACK))
                 quo[(g, mh)] = tile
@@ -324,7 +339,9 @@ def tile_list_quota_penalty_scores_kernel(
                     if (g, t, mh) not in accs2:
                         second_pass(g, t, mh, 0)
                     second_pass(g, t, mh, 1)
-                d = ring.tile([P, width], F32, tag="raw", bufs=5, name="d")
+                held = (g, mh, t) == (1, 0, 0)
+                d = ring.tile([P, width], F32, tag="hold11" if held else "raw", bufs=1 if held else 5, name="d",
+                              align_bytes=64)
                 nc.vector.tensor_tensor(out=d[:], in0=accs2[(g, t, mh)][:, c0:c0 + width],
                                         in1=quo[(g, mh)][:, t, c0:c0 + width], op=ALU.subtract)
                 r = ring.tile([P, width], F32, tag="r", bufs=3, name="r")
@@ -337,12 +354,12 @@ def tile_list_quota_penalty_scores_kernel(
                 if t % 2 == 1:
                     nc.sync.dma_start(out=y_out[:, t - 1:t + 1, :], in_=y[:, t - 1:t + 1, :])
             grouped = ring.tile([P, PACK * width], BF16, tag="grp", bufs=3, name="y_grp", align_bytes=64)
-            dst = grouped[:].rearrange("p (c i t) -> p c t i", i=4, t=PACK)
-            srcv = y[:].rearrange("p t (c i) -> p c t i", i=4)
+            dst = grouped[:].rearrange("p (c i t) -> p c i t", i=4, t=PACK)
+            srcv = y[:].rearrange("p t (c i) -> p c i t", i=4)
             nc.vector.tensor_copy(out=dst[:, cast_split:], in_=srcv[:, cast_split:])
             if cast_split > 0:
                 nc.scalar.copy(out=dst[:, :cast_split], in_=srcv[:, :cast_split])
-            codes = ring.tile([P, width], U32, tag="y_c", bufs=4, name="y_c", align_bytes=64)
+            codes = ring.tile([P, width], U32, tag="y_c", bufs=3, name="y_c", align_bytes=64)
             scol = g * T2 + BANK * mh + c0
             nc.vector.quantize_mx(out=codes[:].bitcast(FP8X4), scales=y_s[:, scol:scol + width], in_=grouped[:])
             nc.sync.dma_start(out=out_1[g, :, cols, :].rearrange("p m i -> p (m i)").bitcast(I32),
@@ -350,6 +367,10 @@ def tile_list_quota_penalty_scores_kernel(
 
         finish(0, 0, 0, BANK, (0,), 0)
         finish(1, 0, 0, BANK, (), 0)
+        codes = ring.tile([P, BANK], U32, tag="hold11", bufs=1, name="z_c11", align_bytes=64)
+        scales = keep.tile([P, BANK], U8, name="z_s11", align_bytes=64)
+        nc.vector.quantize_mx(out=codes[:].bitcast(FP8X4), scales=scales[:], in_=z_late[:])
+        z_q[(1, 1)] = (codes, scales)
         finish(0, 1, 0, BANK, (), 0)
         finish(1, 1, 0, BANK // 2, (), 0)
         finish(1, 1, BANK // 2, BANK // 2, (3,), 20)

@@ -61,17 +61,22 @@ def tile_list_quota_penalty_scores_kernel(
         for page in pages:
             nc.vector.memset(page[:], 0.0)
 
-        def load_tab(a):
-            nc.sync.dma_start(out=tab_w[a][:].bitcast(I32),
-                              in_=tab_words[a].rearrange("p t i -> p (t i)").bitcast(I32))
+        def load_tab(a, pieces=1):
+            width = T // pieces
+            for k in range(pieces):
+                cols = slice(width * k, width * (k + 1))
+                nc.sync.dma_start(out=tab_w[a][:].bitcast(I32)[:, cols],
+                                  in_=tab_words[a].rearrange("p t i -> p (t i)").bitcast(I32)[:, cols])
 
         w1_raw = {}
 
-        def load_w1(a, b):
+        def load_w1(a, b, pieces=1):
             last = (a, b) == (passes1 - 1, 1)
             raw = ring.tile([P, PACK, KP], F32, tag="hold_w" if last else "wq", bufs=1 if last else 4, name="w1_raw")
-            nc.sync.dma_start(out=raw[:], in_=w1[KP * a:KP * (a + 1), KP * b:KP * (b + 1)]
-                              .rearrange("(p j) c -> p j c", j=PACK))
+            rows = w1[KP * a:KP * (a + 1), KP * b:KP * (b + 1)].rearrange("(p j) c -> p j c", j=PACK)
+            step = PACK // pieces
+            for k in range(pieces):
+                nc.sync.dma_start(out=raw[:, step * k:step * (k + 1), :], in_=rows[:, step * k:step * (k + 1), :])
             w1_raw[(a, b)] = raw
 
         def load_vec(tile, vec):
@@ -87,16 +92,14 @@ def tile_list_quota_penalty_scores_kernel(
                               in_=w3_scales[:, 4 * q:4 * q + 4, :].bitcast(I32).rearrange("a r n -> r a n"))
 
         nc.sync.dma_start(offs_t[:], offs)
-        load_tab(0)
+        load_tab(0, 2)
         nc.sync.dma_start(out=w3_w[:].bitcast(I32).rearrange("p (a n) -> p a n", a=groups),
                           in_=w3_words.bitcast(I32).rearrange("a p n -> p a n"))
         ident = keep.tile([P, P], F32, name="ident")
         make_identity(nc, ident[:])
         load_vec(least_t, least)
         nc.sync.dma_start(offs2_t[:], offs2)
-        load_vec(lo_t, lo)
-        load_vec(hi_t, hi)
-        load_w1(0, 0)
+        load_w1(0, 0, 2)
         for q in range(4):
             load_tab_scales(q)
         load_tab(1)
@@ -110,6 +113,8 @@ def tile_list_quota_penalty_scores_kernel(
             nc.sync.dma_start(out=raw[:], in_=w1[KP * 2:KP * 3, 256 * hf:256 * (hf + 1)]
                               .rearrange("(p j) c -> p j c", j=PACK))
             w1_last.append(raw)
+        load_vec(lo_t, lo)
+        load_vec(hi_t, hi)
         nc.sync.dma_start(out=wgs_t[:], in_=wgs)
 
         com = {}
@@ -301,10 +306,10 @@ def tile_list_quota_penalty_scores_kernel(
                                     in1=com[(1, u)][:, e, 0:BANK], op=ALU.add)
             if t == PACK - 1:
                 grouped = ring.tile([P, PACK * BANK], BF16, tag="hold6", bufs=1, name="z_grp", align_bytes=64)
-                dst = grouped[:].rearrange("p (m t) -> p m t", t=PACK)
-                srcv = z4[:].rearrange("p t m -> p m t")
-                nc.vector.tensor_copy(out=dst[:, 160:], in_=srcv[:, 160:])
-                nc.scalar.copy(out=dst[:, :160], in_=srcv[:, :160])
+                dst = grouped[:].rearrange("p (c i t) -> p c t i", i=4, t=PACK)
+                srcv = z4[:].rearrange("p t (c i) -> p c t i", i=4)
+                nc.vector.tensor_copy(out=dst[:, 40:], in_=srcv[:, 40:])
+                nc.scalar.copy(out=dst[:, :40], in_=srcv[:, :40])
                 codes = keep.tile([P, BANK], U32, name="z_c10", align_bytes=64)
                 scales = keep.tile([P, BANK], U8, name="z_s10", align_bytes=64)
                 nc.vector.quantize_mx(out=codes[:].bitcast(FP8X4), scales=scales[:], in_=grouped[:])
@@ -354,8 +359,8 @@ def tile_list_quota_penalty_scores_kernel(
                 if t % 2 == 1:
                     nc.sync.dma_start(out=y_out[:, t - 1:t + 1, :], in_=y[:, t - 1:t + 1, :])
             grouped = ring.tile([P, PACK * width], BF16, tag="grp", bufs=3, name="y_grp", align_bytes=64)
-            dst = grouped[:].rearrange("p (c i t) -> p c i t", i=4, t=PACK)
-            srcv = y[:].rearrange("p t (c i) -> p c i t", i=4)
+            dst = grouped[:].rearrange("p (c i t) -> p c t i", i=4, t=PACK)
+            srcv = y[:].rearrange("p t (c i) -> p c t i", i=4)
             nc.vector.tensor_copy(out=dst[:, cast_split:], in_=srcv[:, cast_split:])
             if cast_split > 0:
                 nc.scalar.copy(out=dst[:, :cast_split], in_=srcv[:, :cast_split])
@@ -375,5 +380,6 @@ def tile_list_quota_penalty_scores_kernel(
         finish(1, 1, 0, BANK // 2, (), 0)
         finish(1, 1, BANK // 2, BANK // 2, (3,), 20)
         for q in range(4):
-            nc.sync.dma_start(out=out_2[:, 4 * q:4 * q + 4, :].bitcast(I32).rearrange("g r m -> r g m"),
+            queue = nc.scalar if q % 2 == 0 else nc.sync
+            queue.dma_start(out=out_2[:, 4 * q:4 * q + 4, :].bitcast(I32).rearrange("g r m -> r g m"),
                               in_=y_s[32 * q:32 * q + 4, :].bitcast(I32).rearrange("r (g m) -> r g m", g=groups))

from contextlib import ExitStack

import concourse.mybir as mybir
from concourse.masks import make_identity

K, T, S, T2, H, N = 1536, 2048, 512, 1024, 1024, 1024
FLOPS = 2 * K * H * S + 2 * H * N * T2

F32 = mybir.dt.float32
BF16 = mybir.dt.bfloat16
I32 = mybir.dt.int32
U32 = mybir.dt.uint32
U16 = mybir.dt.uint16
U8 = mybir.dt.uint8
FP8X4 = mybir.dt.float8_e4m3fn_x4
FP4X4 = mybir.dt.float4_e2m1fn_x4
ALU = mybir.AluOpType
ACT = mybir.ActivationFunctionType

P = 128
PACK = 4
KP = P * PACK
BANK = 512
PAGES = 4


def tile_list_quota_penalty_scores_kernel(
    tc, tab_words, tab_scales, offs, w1, lo, hi, wgs, offs2, committed,
    w3_words, w3_scales, quota, least, out_0, out_1, out_2,
):
    nc = tc.nc
    passes1 = K // KP
    groups = H // KP
    halves = T2 // BANK

    with ExitStack() as ctx:
        keep = ctx.enter_context(tc.tile_pool(name="keep", bufs=1))
        ring = ctx.enter_context(tc.tile_pool(name="ring", bufs=1))
        psum = ctx.enter_context(tc.psum_pool(name="psum", bufs=1))

        offs_t = keep.tile([P, S // 16], U16, name="offs_t")
        offs2_t = keep.tile([P, S // 16], U16, name="offs2_t")
        tab_s = keep.tile([P, T], U8, name="tab_s", align_bytes=64)
        w3_s = keep.tile([P, groups * N], U8, name="w3_s", align_bytes=64)
        w3_w = keep.tile([P, groups * 2 * N], U8, name="w3_w", align_bytes=64)
        w3_sp = keep.tile([P, groups * N], U8, name="w3_sp", align_bytes=64)
        w3_wp = keep.tile([P, groups * 2 * N], U8, name="w3_wp", align_bytes=64)
        lo_t = keep.tile([P, 8], F32, name="lo_t")
        hi_t = keep.tile([P, 8], F32, name="hi_t")
        least_t = keep.tile([P, 8], F32, name="least_t")
        nleast_t = keep.tile([P, 8], F32, name="nleast_t")
        wgs_t = keep.tile([P, S], F32, name="wgs_t")
        tab_w = [keep.tile([P, T], U32, name="tab_w%d" % a, align_bytes=64) for a in range(passes1)]
        v_w = [keep.tile([P, S], U32, name="v_w%d" % a, align_bytes=64) for a in range(passes1)]
        v_s = keep.tile([P, S], U8, name="v_s", align_bytes=64)
        pages = [keep.tile([P, T2], F32, name="page%d" % i) for i in range(PAGES)]
        y_s = keep.tile([P, groups * T2], U8, name="y_s", align_bytes=64)

        nc.vector.memset(tab_s[:].bitcast(I32), 0)
        nc.vector.memset(w3_s[:].bitcast(I32), 0)
        for page in pages:
            nc.vector.memset(page[:], 0.0)

        def load_tab(a, pieces=1):
            width = T // pieces
            for k in range(pieces):
                cols = slice(width * k, width * (k + 1))
                nc.sync.dma_start(out=tab_w[a][:].bitcast(I32)[:, cols],
                                  in_=tab_words[a].rearrange("p t i -> p (t i)").bitcast(I32)[:, cols])

        w1_raw = {}

        def load_w1(a, b, pieces=1):
            last = (a, b) == (passes1 - 1, 1)
            raw = ring.tile([P, PACK, KP], F32, tag="hold_w" if last else "wq", bufs=1 if last else 4, name="w1_raw")
            rows = w1[KP * a:KP * (a + 1), KP * b:KP * (b + 1)].rearrange("(p j) c -> p j c", j=PACK)
            step = PACK // pieces
            for k in range(pieces):
                nc.sync.dma_start(out=raw[:, step * k:step * (k + 1), :], in_=rows[:, step * k:step * (k + 1), :])
            w1_raw[(a, b)] = raw

        def load_vec(tile, vec):
            nc.sync.dma_start(out=tile[:].rearrange("p (b t) -> p b t", t=PACK),
                              in_=vec.rearrange("(b p t) -> p b t", p=P, t=PACK))

        def load_tab_scales(q):
            nc.sync.dma_start(out=tab_s[32 * q:32 * q + 4 * passes1, :].bitcast(I32),
                              in_=tab_scales[:, 4 * q:4 * q + 4, :].bitcast(I32))

        def load_w3_scales(q):
            nc.sync.dma_start(out=w3_s[32 * q:32 * q + 4, :].bitcast(I32).rearrange("r (a n) -> r a n", a=groups),
                              in_=w3_scales[:, 4 * q:4 * q + 4, :].bitcast(I32).rearrange("a r n -> r a n"))

        nc.sync.dma_start(offs_t[:], offs)
        load_tab(0, 2)
        nc.sync.dma_start(out=w3_w[:].bitcast(I32).rearrange("p (a n) -> p a n", a=groups),
                          in_=w3_words.bitcast(I32).rearrange("a p n -> p a n"))
        ident = keep.tile([P, P], F32, name="ident")
        make_identity(nc, ident[:])
        load_vec(least_t, least)
        nc.sync.dma_start(offs2_t[:], offs2)
        load_w1(0, 0, 2)
        for q in range(4):
            load_tab_scales(q)
        load_tab(1)
        for q in range(4):
            load_w3_scales(q)
        load_w1(1, 0)
        load_tab(2)
        w1_last = []
        for hf in range(2):
            raw = ring.tile([P, PACK, KP // 2], F32, tag="wl", bufs=2, name="w1_last")
            nc.sync.dma_start(out=raw[:], in_=w1[KP * 2:KP * 3, 256 * hf:256 * (hf + 1)]
                              .rearrange("(p j) c -> p j c", j=PACK))
            w1_last.append(raw)
        load_vec(lo_t, lo)
        load_vec(hi_t, hi)
        nc.sync.dma_start(out=wgs_t[:], in_=wgs)

        com = {}

        def load_com(b, u):
            tile = ring.tile([P, 2, T2], F32, tag="cy", bufs=4, name="com")
            nc.sync.dma_start(out=tile[:], in_=committed[KP * b:KP * (b + 1), :]
                              .rearrange("(p t) m -> p t m", t=PACK)[:, 2 * u:2 * u + 2, :])
            com[(b, u)] = tile

        load_com(0, 0)
        for a in range(passes1):
            load_w1(a, 1)
        load_com(0, 1)
        load_com(1, 0)
        load_com(1, 1)

        nc.scalar.activation(out=nleast_t[:], in_=least_t[:], func=ACT.Identity, scale=-1.0)

        def gather(a):
            nc.vector.tensor_copy(out=v_w[a][:], in_=tab_w[a][:].indirect(offs_t[:]))

        w1_q = {}

        def quant_w1(a, b, split):
            tag = {(0, 1): "hold2", (2, 1): "hold3"}.get((a, b), "grp")
            grouped = ring.tile([P, PACK * KP], BF16, tag=tag, bufs=3 if tag == "grp" else 1, name="w1_grp", align_bytes=64)
            dst = grouped[:].rearrange("p (t m j) -> p m t j", t=PACK, j=PACK)
            srcv = w1_raw[(a, b)][:].rearrange("p j (m t) -> p m t j", t=PACK)
            if split < P:
                nc.vector.tensor_copy(out=dst[:, split:], in_=srcv[:, split:])
            nc.scalar.copy(out=dst[:, :split], in_=srcv[:, :split])
            codes = keep.tile([P, KP], U32, name="w1_c%d%d" % (a, b), align_bytes=64)
            scales = keep.tile([P, KP], U8, name="w1_s%d%d" % (a, b), align_bytes=64)
            nc.vector.quantize_mx(out=codes[:].bitcast(FP8X4), scales=scales[:], in_=grouped[:])
            w1_q[(a, b)] = (codes, scales)

        def first_pass(acc, a, b, t):
            codes, scales = w1_q[(a, b)]
            nc.tensor.matmul_mx(out=acc[:], lhsT=codes[:, P * t:P * (t + 1)].bitcast(FP8X4),
                                lhsT_scale=scales[:, P * t:P * (t + 1)],
                                rhs=v_w[a][:].bitcast(FP8X4), rhs_scale=v_s[4 * a:P, :],
                                start=(a == 0), stop=(a == passes1 - 1))

        gather(0)
        nc.vector.tensor_copy(
            out=w3_wp[:].rearrange("p (g t m e) -> p g t m e", t=PACK, m=P, e=2),
            in_=w3_w[:].rearrange("p (g m t e) -> p g t m e", t=PACK, m=P, e=2))
        nc.vector.tensor_copy(out=v_s[:], in_=tab_s[:].indirect(offs_t[:]))
        quant_w1(0, 0, P)
        gather(1)
        nc.vector.tensor_copy(
            out=w3_sp[:].rearrange("p (g t m) -> p g t m", t=PACK, m=P),
            in_=w3_s[:].rearrange("p (g m t) -> p g t m", t=PACK, m=P))
        quant_w1(1, 0, P)
        gather(2)
        grouped = ring.tile([P, PACK * KP], BF16, tag="hold2", bufs=1, name="w1_grp", align_bytes=64)
        dst = grouped[:].rearrange("p (t m j) -> p m t j", t=PACK, j=PACK)
        src0 = w1_last[0][:].rearrange("p j (m t) -> p m t j", t=PACK)
        src1 = w1_last[1][:].rearrange("p j (m t) -> p m t j", t=PACK)
        nc.scalar.copy(out=dst[:, :64], in_=src0)
        nc.vector.tensor_copy(out=dst[:, 84:], in_=src1[:, 20:])
        nc.scalar.copy(out=dst[:, 64:84], in_=src1[:, :20])
        codes = keep.tile([P, KP], U32, name="w1_c20", align_bytes=64)
        scales = keep.tile([P, KP], U8, name="w1_s20", align_bytes=64)
        for lo_c, hi_c in ((0, P), (P, 2 * P), (2 * P, KP)):
            nc.vector.quantize_mx(out=codes[:, lo_c:hi_c].bitcast(FP8X4), scales=scales[:, lo_c:hi_c],
                                  in_=grouped[:, PACK * lo_c:PACK * hi_c])
        w1_q[(2, 0)] = (codes, scales)

        z_q = {}
        accs2 = {}
        bank_tags = ["C", "C", "A", "A", "A", "A", "B", "B"]

        def bank(tag, name):
            return psum.tile([P, BANK], F32, tag=tag, bufs=4 if tag == "A" else 2, name=name)

        def second_pass(g, t, mh, b):
            if b == 0:
                accs2[(g, t, mh)] = bank(bank_tags[len(accs2) % 8], "acc2")
            codes, scales = z_q[(b, mh)]
            col = (b * groups + g) * KP + t * P
            nc.tensor.matmul_mx(out=accs2[(g, t, mh)][:], lhsT=w3_wp[:, 2 * col:2 * (col + P)].bitcast(FP4X4),
                                lhsT_scale=w3_sp[:, col:col + P],
                                rhs=codes[:].bitcast(FP8X4), rhs_scale=scales[:],
                                start=(b == 0), stop=(b == groups - 1))

        raws = {}

        def evac(i, acc):
            raw = ring.tile([P, S], F32, tag="raw", bufs=5, name="raw", align_bytes=64)
            nc.scalar.copy(out=raw[:], in_=acc[:])
            raws[i] = raw

        def quant_z0(mq):
            c0 = ring.tile([P, BANK], U32, tag="hold%d" % (5 + mq), bufs=1, name="z_c0", align_bytes=64)
            s0 = keep.tile([P, BANK], U8, name="z_s0%d" % mq, align_bytes=64)
            nc.vector.quantize_mx(out=c0[:].bitcast(FP8X4), scales=s0[:], in_=z_q[(0, mq)][:])
            z_q[(0, mq)] = (c0, s0)

        def post(i):
            tag = {3: "hold3", 6: "hold5"}.get(i, "h")
            h = ring.tile([P, S], F32, tag=tag, bufs=3 if tag == "h" else 1, name="h", align_bytes=64)
            raw = raws[i]
            nc.vector.tensor_scalar(out=h[:], in0=raw[:], scalar1=lo_t[:, i:i + 1], scalar2=hi_t[:, i:i + 1],
                                    op0=ALU.max, op1=ALU.min)
            nc.vector.tensor_tensor(out=pages[i % PAGES][:].indirect(offs2_t[:]), in0=h[:], in1=wgs_t[:], op=ALU.mult)

        def turn(dst, srcv, start, stop):
            nc.tensor.matmul(out=dst, lhsT=srcv, rhs=ident[:], start=start, stop=stop, is_transpose=True)

        accs = [bank("A", "acc1") for t in range(PACK)]
        for a in range(passes1):
            for t in range(PACK):
                first_pass(accs[t], a, 0, t)
        raws[0] = accs[0]
        for t in range(1, PACK):
            evac(t, accs[t])
        z_t = {}
        sums = {}

        def block(jj, j):
            return slice(P * (2 * jj + j), P * (2 * jj + j + 1))

        def turn_com(b, u, jjs):
            for jj in jjs:
                sums[jj] = bank("A", "sums")
                for j in range(2):
                    for e in range(2):
                        turn(sums[jj][:, P * (2 * j + e):P * (2 * j + e + 1)], com[(b, u)][:, e, block(jj, j)],
                             j == 0 and e == 0, False)

        def turn_page(b, u, e, jjs):
            page = pages[(PACK * b + 2 * u + e) % PAGES]
            for jj in jjs:
                for j in range(2):
                    turn(sums[jj][:, P * (2 * j + e):P * (2 * j + e + 1)], page[:, block(jj, j)],
                         False, j == 1 and e == 1)

        def round_sums(b, u, jjs):
            first = (b, u) == (0, 0)
            zt = ring.tile([P, BANK * len(jjs)], BF16, tag="hold_w" if first else "zt", bufs=1 if first else 2, name="zt")
            for k, jj in enumerate(jjs):
                part = zt[:, BANK * k:BANK * (k + 1)]
                nc.scalar.copy(out=part.rearrange("m (j p e) -> m j p e", j=2, e=2),
                               in_=sums[jj][:].rearrange("m (j e p) -> m j p e", j=2, e=2))
                z_t[(u, jj)] = part

        def turn_back(mh):
            grouped = ring.tile([P, PACK * BANK], BF16, tag="grp", bufs=3, name="z_grp", align_bytes=64)
            for jh in range(2):
                jj = 2 * mh + jh
                words = bank("B", "words")
                for u in range(2):
                    for j in range(2):
                        turn(words[:, P * (2 * u + j):P * (2 * u + j + 1)],
                             z_t[(u, jj)].bitcast(F32)[:, P * j:P * (j + 1)], True, True)
                nc.scalar.copy(out=grouped[:].bitcast(F32)[:, BANK * jh:BANK * (jh + 1)].rearrange("p (m u) -> p m u", u=2),
                               in_=words[:].rearrange("p (u m) -> p m u", u=2))
            return grouped

        for u in range(2):
            for e in range(2):
                t = 2 * u + e
                if t == 2:
                    quant_w1(0, 1, P)
                if t == 3:
                    quant_w1(1, 1, P)
                    quant_w1(2, 1, P)
                    for t1 in range(PACK):
                        acc = bank("C", "acc1")
                        for a in range(passes1):
                            first_pass(acc, a, 1, t1)
                        evac(PACK + t1, acc)
                post(t)
            turn_com(0, u, range(4))
            for e in range(2):
                turn_page(0, u, e, range(4))
            round_sums(0, u, range(4))
        for mh in range(halves):
            z_q[(0, mh)] = turn_back(mh)

        z4 = keep.tile([P, PACK, BANK], BF16, name="z4")
        late = (2, 3)
        for t in range(PACK):
            u, e = divmod(t, 2)
            post(PACK + t)
            nc.vector.tensor_tensor(out=z4[:, t, :], in0=pages[(PACK + t) % PAGES][:, 0:BANK],
                                    in1=com[(1, u)][:, e, 0:BANK], op=ALU.add)
            if t == PACK - 1:
                grouped = ring.tile([P, PACK * BANK], BF16, tag="hold6", bufs=1, name="z_grp", align_bytes=64)
                dst = grouped[:].rearrange("p (c i t) -> p c t i", i=4, t=PACK)
                srcv = z4[:].rearrange("p t (c i) -> p c t i", i=4)
                nc.vector.tensor_copy(out=dst[:, 40:], in_=srcv[:, 40:])
                nc.scalar.copy(out=dst[:, :40], in_=srcv[:, :40])
                codes = keep.tile([P, BANK], U32, name="z_c10", align_bytes=64)
                scales = keep.tile([P, BANK], U8, name="z_s10", align_bytes=64)
                nc.vector.quantize_mx(out=codes[:].bitcast(FP8X4), scales=scales[:], in_=grouped[:])
                z_q[(1, 0)] = (codes, scales)
                quant_z0(1)
            if e == 0:
                turn_com(1, u, late)
            turn_page(1, u, e, late)
            if e == 1:
                round_sums(1, u, late)
            if t == 2:
                quant_z0(0)
                for t2 in range(PACK):
                    second_pass(0, t2, 0, 0)
        z_late = turn_back(1)

        quo = {}
        for mh in range(halves):
            for g in range(groups):
                tile = ring.tile([P, PACK, BANK], F32, tag="wq", bufs=4, name="quo")
                nc.sync.dma_start(out=tile[:], in_=quota[KP * g:KP * (g + 1), BANK * mh:BANK * (mh + 1)]
                                  .rearrange("(p t) m -> p t m", t=PACK))
                quo[(g, mh)] = tile

        def finish(g, mh, c0, width, on_vector, cast_split):
            cols = slice(BANK * mh + c0, BANK * mh + c0 + width)
            y = ring.tile([P, PACK, width], F32, tag="cy", bufs=4, name="y")
            y_out = out_0[KP * g:KP * (g + 1), cols].rearrange("(p t) m -> p t m", t=PACK)
            for t in range(PACK):
                i = g * PACK + t
                if c0 == 0:
                    if (g, t, mh) not in accs2:
                        second_pass(g, t, mh, 0)
                    second_pass(g, t, mh, 1)
                held = (g, mh, t) == (1, 0, 0)
                d = ring.tile([P, width], F32, tag="hold11" if held else "raw", bufs=1 if held else 5, name="d",
                              align_bytes=64)
                nc.vector.tensor_tensor(out=d[:], in0=accs2[(g, t, mh)][:, c0:c0 + width],
                                        in1=quo[(g, mh)][:, t, c0:c0 + width], op=ALU.subtract)
                r = ring.tile([P, width], F32, tag="r", bufs=3, name="r")
                if t in on_vector:
                    nc.vector.tensor_scalar(out=r[:], in0=d[:], scalar1=least_t[:, i:i + 1], scalar2=None, op0=ALU.max)
                    nc.scalar.activation(out=y[:, t, :], in_=r[:], func=ACT.Square)
                else:
                    nc.scalar.activation(out=r[:], in_=d[:], func=ACT.Relu, bias=nleast_t[:, i:i + 1])
                    nc.scalar.activation(out=y[:, t, :], in_=r[:], func=ACT.Square, bias=least_t[:, i:i + 1])
                if t % 2 == 1:
                    nc.sync.dma_start(out=y_out[:, t - 1:t + 1, :], in_=y[:, t - 1:t + 1, :])
            grouped = ring.tile([P, PACK * width], BF16, tag="grp", bufs=3, name="y_grp", align_bytes=64)
            dst = grouped[:].rearrange("p (c i t) -> p c t i", i=4, t=PACK)
            srcv = y[:].rearrange("p t (c i) -> p c t i", i=4)
            nc.vector.tensor_copy(out=dst[:, cast_split:], in_=srcv[:, cast_split:])
            if cast_split > 0:
                nc.scalar.copy(out=dst[:, :cast_split], in_=srcv[:, :cast_split])
            codes = ring.tile([P, width], U32, tag="y_c", bufs=3, name="y_c", align_bytes=64)
            scol = g * T2 + BANK * mh + c0
            nc.vector.quantize_mx(out=codes[:].bitcast(FP8X4), scales=y_s[:, scol:scol + width], in_=grouped[:])
            nc.sync.dma_start(out=out_1[g, :, cols, :].rearrange("p m i -> p (m i)").bitcast(I32),
                              in_=codes[:].bitcast(I32))

        finish(0, 0, 0, BANK, (0,), 0)
        finish(1, 0, 0, BANK, (), 0)
        codes = ring.tile([P, BANK], U32, tag="hold11", bufs=1, name="z_c11", align_bytes=64)
        scales = keep.tile([P, BANK], U8, name="z_s11", align_bytes=64)
        nc.vector.quantize_mx(out=codes[:].bitcast(FP8X4), scales=scales[:], in_=z_late[:])
        z_q[(1, 1)] = (codes, scales)
        finish(0, 1, 0, BANK, (), 0)
        finish(1, 1, 0, BANK // 2, (), 0)
        finish(1, 1, BANK // 2, BANK // 2, (3,), 20)
        for q in range(4):
            queue = nc.scalar if q % 2 == 0 else nc.sync
            queue.dma_start(out=out_2[:, 4 * q:4 * q + 4, :].bitcast(I32).rearrange("g r m -> r g m"),
                              in_=y_s[32 * q:32 * q + 4, :].bitcast(I32).rearrange("r (g m) -> r g m", g=groups))
